import numpy as np
import ml_dtypes


def mxq(x, axis, fmt="e4m3"):
    dtype, down = {"e4m3": (ml_dtypes.float8_e4m3fn, 7), "e5m2": (ml_dtypes.float8_e5m2, 14)}[fmt]
    v = np.moveaxis(np.asarray(x, np.float32).astype(ml_dtypes.bfloat16).astype(np.float64), axis, -1)
    blocks = v.reshape(v.shape[:-1] + (-1, 32))
    amax = np.abs(blocks).max(-1, keepdims=True)
    byte = np.maximum(np.where(amax > 0, np.frexp(amax)[1] - 1 + 127, 0) - down, 1)
    scale = np.exp2(byte - 127.0)
    codes = (blocks / scale).astype(np.float32).astype(dtype).astype(np.float64)
    return np.moveaxis((codes * scale).reshape(v.shape), -1, axis)


WIDE = False


def mx_kscale(k):
    if not WIDE:
        return np.ones(k)
    levels = np.array([10, -10, 5, -5, 0])
    if k % 512:
        return np.exp2(np.random.permutation(np.resize(levels, k // 32))).repeat(32)
    a = np.empty((k // 512, 16))
    for p in range(k // 512):
        a[p, :8] = np.random.permutation(np.resize(levels, 8))
        for g in range(8):
            far = levels[np.abs(levels - a[p, g]) >= 10]
            a[p, g + 8] = far[np.random.randint(len(far))]
    return np.exp2(a.ravel()).repeat(32)


def f64(x):
    return np.asarray(x).astype(np.float64)


E2M1 = np.array([0.0, 0.5, 1.0, 1.5, 2.0, 3.0, 4.0, 6.0, -0.0, -0.5, -1.0, -1.5, -2.0, -3.0, -4.0, -6.0])


def pack_weight(w, fmt):
    k, n = w.shape
    w = f64(np.asarray(w, np.float32).astype(ml_dtypes.bfloat16)).reshape(k // 32, 32, n)
    amax = np.abs(w).max(1)
    if fmt == "e4m3":
        byte = np.frexp(amax)[1] - 1 + 127 - 7
    else:
        mant, ex = np.frexp(amax / 6.0)
        byte = np.where(mant > 0.5, ex, ex - 1) + 127
    byte = np.clip(np.where(amax > 0, byte, 1), 1, 254)
    scaled = (w * np.exp2(127.0 - byte)[:, None, :]).reshape(k, n).astype(np.float32)
    by_word = np.ascontiguousarray(scaled.reshape(k // 512, 128, 4, n).transpose(0, 1, 3, 2))
    if fmt == "e4m3":
        words = by_word.astype(ml_dtypes.float8_e4m3fn).view(np.uint8)
    else:
        c = by_word.astype(ml_dtypes.float4_e2m1fn).view(np.uint8) & 0xF
        words = (c[..., 0::2] | (c[..., 1::2] << 4)).reshape(k // 512, 128, 2 * n)
    return np.ascontiguousarray(words), np.ascontiguousarray(byte.astype(np.uint8).reshape(k // 512, 16, n))


def unpack_weight(words, scales, fmt):
    g, _, n = scales.shape
    words = np.ascontiguousarray(words).reshape(g, 128, n, -1)
    if fmt == "e4m3":
        vals = words.view(ml_dtypes.float8_e4m3fn).astype(np.float64)
    else:
        nib = np.empty((g, 128, n, 4), np.uint8)
        nib[..., 0::2] = words & 0xF
        nib[..., 1::2] = words >> 4
        vals = E2M1[nib]
    vals = vals * np.repeat(np.exp2(scales.astype(np.float64) - 127.0), 8, axis=1)[..., None]
    return vals.transpose(0, 1, 3, 2).reshape(g * 512, n)


def planes(y):
    n, m = y.shape
    v = y.astype(np.float32).astype(ml_dtypes.bfloat16).astype(np.float64).reshape(n // 32, 32, m)
    top = np.abs(v).max(1)
    byte = np.clip(np.where(top > 0, np.frexp(top)[1] - 1 + 127 - 7, 1), 1, 254)
    codes = (v * np.exp2(127.0 - byte)[:, None, :]).reshape(n, m).astype(np.float32).astype(ml_dtypes.float8_e4m3fn).view(np.uint8)
    words = codes.reshape(n // 512, 128, 4, m).transpose(0, 1, 3, 2)
    return np.ascontiguousarray(words), np.ascontiguousarray(byte.astype(np.uint8).reshape(n // 512, 16, m))


K, M, T = 1536, 512, 1536


def setup_inputs():
    n = np.random.standard_normal
    s = mx_kscale(K)[:, None]
    p_w4 = pack_weight(n((K, M)) / np.sqrt(K) / s ** 2, "e2m1")
    p_w8 = pack_weight(n((K, M)) / np.sqrt(K) / s, "e4m3")
    return {
        "x": (n((K, T)) * s).astype(np.float32),
        "w4_words": p_w4[0],
        "w4_scales": p_w4[1],
        "w8_words": p_w8[0],
        "w8_scales": p_w8[1],
    }


def reference(x, w4_words, w4_scales, w8_words, w8_scales):
    xa_, xb_ = mxq(f64(x) ** 2, 0, "e4m3"), mxq(f64(x), 0, "e4m3")
    w4_ = unpack_weight(w4_words, w4_scales, "e2m1")
    w8_ = unpack_weight(w8_words, w8_scales, "e4m3")
    y = xa_.T @ w4_ + xb_.T @ w8_
    out_0 = np.maximum(y, 0.0) ** 2
    return (out_0,) + planes(out_0)

@@ -1,0 +1,270 @@
+from contextlib import ExitStack
+
+import concourse.mybir as mybir
+
+K, N, T = 1536, 512, 1536
+FLOPS = 2 * 2 * K * N * T
+
+F32 = mybir.dt.float32
+BF16 = mybir.dt.bfloat16
+I32 = mybir.dt.int32
+U8 = mybir.dt.uint8
+FP8X4 = mybir.dt.float8_e4m3fn_x4
+FP4X4 = mybir.dt.float4_e2m1fn_x4
+ACT = mybir.ActivationFunctionType
+ALU = mybir.AluOpType
+
+P = 128
+PACK = 4
+SPAN = P * PACK
+PASSES = K // SPAN
+TILES = T // SPAN
+UNITS = PASSES * TILES
+FIRST_PIECES = (128, 128, 256)
+TAIL_VECTOR_COLS = 320
+W8_ROW = 4
+
+
+def tile_mix_feat_tm_quadpl_relu2_kernel(
+    tc, x, w4_words, w4_scales, w8_words, w8_scales, out_0, out_1, out_2
+):
+    nc = tc.nc
+    with ExitStack() as ctx:
+        keep = ctx.enter_context(tc.tile_pool(name="keep", bufs=1))
+        stage = ctx.enter_context(tc.tile_pool(name="stage", bufs=3))
+        codes_pool = ctx.enter_context(tc.tile_pool(name="codes", bufs=5))
+        psum = ctx.enter_context(tc.psum_pool(name="psum", bufs=2))
+        ctx.enter_context(tc.manual_schedule())
+
+        w_planes = keep.tile([P, PASSES * N], U8, align_bytes=64)
+        zero_seed = keep.tile([P, 8], F32)
+        zero_bias = keep.tile([P, 8], F32)
+        nc.vector.memset(zero_seed[:], 0.0)
+        nc.vector.memset(w_planes[:].bitcast(I32), 0)
+        nc.scalar.activation(out=zero_bias[:], in_=zero_seed[:], func=ACT.Square)
+        bias = zero_bias[:, 0:1]
+
+        def load_scales(scales, row0):
+            for q in range(4):
+                rows = w_planes[32 * q + row0 : 32 * q + row0 + 4, :]
+                nc.sync.dma_start(
+                    out=rows.bitcast(I32).rearrange("r (g n) -> r g n", g=PASSES),
+                    in_=scales[:, 4 * q : 4 * q + 4, :].bitcast(I32).rearrange("g r n -> r g n"),
+                )
+
+        raw = {}
+        w4 = {}
+        w8 = {}
+
+        def load_x(u):
+            tile_t, g = divmod(u, PASSES)
+            widths = FIRST_PIECES if u == 0 else (SPAN,)
+            pieces = []
+            c0 = 0
+            for n_piece, width in enumerate(widths):
+                piece = keep.tile([P, PACK, width], F32, name="x_%d_%d" % (u, n_piece))
+                cols = slice(tile_t * SPAN + c0, tile_t * SPAN + c0 + width)
+                nc.sync.dma_start(
+                    out=piece[:],
+                    in_=x[g * SPAN : (g + 1) * SPAN, cols].rearrange("(p j) w -> p j w", j=PACK),
+                )
+                pieces.append((piece, c0 // PACK, width // PACK))
+                c0 = c0 + width
+            raw[u] = pieces
+
+        def load_w8(g):
+            w8[g] = keep.tile([P, N], I32, name="w8_%d" % g, align_bytes=64)
+            nc.sync.dma_start(out=w8[g][:], in_=w8_words[g].rearrange("p n i -> p (n i)").bitcast(I32))
+
+        def load_w4(g):
+            w4[g] = keep.tile([P, 2 * N], U8, name="w4_%d" % g, align_bytes=64)
+            nc.sync.dma_start(out=w4[g][:].bitcast(I32), in_=w4_words[g].bitcast(I32))
+
+        load_x(0)
+        load_x(1)
+        load_scales(w8_scales, W8_ROW)
+        load_w8(0)
+        load_x(2)
+        load_scales(w4_scales, 0)
+        load_w4(0)
+        load_w8(1)
+        load_x(3)
+        load_w4(1)
+        load_w8(2)
+        load_w4(2)
+        for u in range(4, UNITS):
+            load_x(u)
+
+        lin_bf, sq_bf, lin_q, sq_q, acc, rel, res, res_bf = {}, {}, {}, {}, {}, {}, {}, {}
+        res_plane = keep.tile([P, TILES * N], U8, align_bytes=64)
+
+        def dealt(dst, banks):
+            return dst[:].rearrange("p (r m j) -> p m j r", r=banks, j=PACK)
+
+        def by_group(piece):
+            return piece[:].rearrange("p j (m r) -> p m j r", r=PACK)
+
+        def round_lin(u):
+            lin_bf[u] = stage.tile([P, PACK * SPAN], BF16, name="lin_bf", align_bytes=64)
+            for piece, m0, m_n in raw[u]:
+                nc.vector.tensor_copy(out=dealt(lin_bf[u], PACK)[:, m0 : m0 + m_n], in_=by_group(piece))
+
+        def square(u, r0=0, r_n=PACK):
+            sq_bf[u, r0] = stage.tile([P, r_n * SPAN], BF16, name="sq_bf", align_bytes=64)
+            for piece, m0, m_n in raw[u]:
+                nc.scalar.activation(
+                    out=dealt(sq_bf[u, r0], r_n)[:, m0 : m0 + m_n],
+                    in_=by_group(piece)[:, :, :, r0 : r0 + r_n],
+                    func=ACT.Square,
+                    bias=bias,
+                )
+
+        def quantize(src, width, name):
+            words = codes_pool.tile([P, width], I32, name=name + "_words", align_bytes=64)
+            plane = codes_pool.tile([P, width], U8, name=name + "_plane", align_bytes=64)
+            nc.vector.quantize_mx(out=words[:].bitcast(FP8X4), scales=plane[:], in_=src[:])
+            return words, plane
+
+        def quant_lin(u):
+            lin_q[u] = quantize(lin_bf[u], SPAN, "lin")
+
+        def quant_sq(u, r0=0, r_n=PACK):
+            sq_q[u, r0] = quantize(sq_bf[u, r0], r_n * P, "sq")
+
+        def mm_lin(u):
+            tile_t, g = divmod(u, PASSES)
+            words, plane = lin_q[u]
+            for r in range(PACK):
+                if g == 0:
+                    acc[tile_t, r] = psum.tile([P, N], F32, name="acc%d" % r)
+                cols = slice(r * P, (r + 1) * P)
+                nc.tensor.matmul_mx(
+                    out=acc[tile_t, r][:],
+                    lhsT=words[:, cols].bitcast(FP8X4),
+                    lhsT_scale=plane[:, cols],
+                    rhs=w8[g][:].bitcast(FP8X4),
+                    rhs_scale=w_planes[W8_ROW:, g * N : (g + 1) * N],
+                    start=(g == 0),
+                    stop=False,
+                )
+
+        def mm_sq(u, r0=0, r_n=PACK):
+            tile_t, g = divmod(u, PASSES)
+            words, plane = sq_q[u, r0]
+            for r in range(r_n):
+                cols = slice(r * P, (r + 1) * P)
+                nc.tensor.matmul_mx(
+                    out=acc[tile_t, r0 + r][:],
+                    lhsT=words[:, cols].bitcast(FP8X4),
+                    lhsT_scale=plane[:, cols],
+                    rhs=w4[g][:].bitcast(FP4X4),
+                    rhs_scale=w_planes[:, g * N : (g + 1) * N],
+                    start=False,
+                    stop=(g == PASSES - 1),
+                )
+
+        def open_result(tile_t):
+            rel[tile_t] = stage.tile([P, PACK * N], F32, name="rel", bufs=2)
+            res[tile_t] = keep.tile([P, PACK * N], F32, name="res_%d" % tile_t)
+            res_bf[tile_t] = stage.tile([P, PACK * N], BF16, name="res_bf", bufs=2, align_bytes=64)
+
+        def relu_scalar(tile_t, r):
+            nc.scalar.activation(out=rel[tile_t][:, r * N : (r + 1) * N], in_=acc[tile_t, r][:], func=ACT.Relu, bias=bias)
+
+        def relu_vector(tile_t, r):
+            nc.vector.tensor_scalar(
+                out=rel[tile_t][:, r * N : (r + 1) * N], in0=acc[tile_t, r][:], scalar1=0.0, scalar2=None, op0=ALU.max
+            )
+
+        def store_rows(tile_t, r0, r_n):
+            rows = out_0[tile_t * SPAN : (tile_t + 1) * SPAN, :].rearrange("(p r) n -> p (r n)", r=PACK)
+            cols = slice(r0 * N, (r0 + r_n) * N)
+            nc.sync.dma_start(out=rows[:, cols], in_=res[tile_t][:, cols])
+
+        def finish_scalar(tile_t, r0, r_n):
+            cols = slice(r0 * N, (r0 + r_n) * N)
+            nc.scalar.activation(out=res[tile_t][:, cols], in_=rel[tile_t][:, cols], func=ACT.Square, bias=bias)
+            store_rows(tile_t, r0, r_n)
+
+        def finish_vector(tile_t, r0, r_n):
+            cols = slice(r0 * N, (r0 + r_n) * N)
+            nc.vector.tensor_tensor(
+                out=res[tile_t][:, cols], in0=rel[tile_t][:, cols], in1=rel[tile_t][:, cols], op=ALU.mult
+            )
+            store_rows(tile_t, r0, r_n)
+
+        def round_result(tile_t, n0, n1, copy):
+            src = res[tile_t][:].rearrange("p (r c e) -> p c r e", r=PACK, e=PACK)
+            dst = res_bf[tile_t][:].rearrange("p (c e r) -> p c r e", r=PACK, e=PACK)
+            copy(out=dst[:, n0 // PACK : n1 // PACK], in_=src[:, n0 // PACK : n1 // PACK])
+
+        def quant_result(tile_t, n0, n1):
+            words = stage.tile([P, n1 - n0], I32, name="res_words", align_bytes=64)
+            nc.vector.quantize_mx(
+                out=words[:].bitcast(FP8X4),
+                scales=res_plane[:, tile_t * N + n0 : tile_t * N + n1],
+                in_=res_bf[tile_t][:, PACK * n0 : PACK * n1],
+            )
+            rows = out_1[tile_t].rearrange("p n i -> p (n i)").bitcast(I32)
+            nc.sync.dma_start(out=rows[:, n0:n1], in_=words[:])
+
+        last = UNITS - 1
+        half = N // 2
+        for u in range(last):
+            done = u // PASSES - 1
+            phase = u % PASSES
+            round_lin(u)
+            square(u)
+            if u > 0:
+                quant_sq(u - 1)
+                mm_sq(u - 1)
+            if done == 0 and phase == 2:
+                quant_result(done, 0, N)
+            quant_lin(u)
+            mm_lin(u)
+            if done >= 0 and phase == 0:
+                open_result(done)
+                relu_scalar(done, 0)
+                relu_scalar(done, 1)
+                relu_vector(done, 2)
+                relu_vector(done, 3)
+                finish_scalar(done, 0, 2)
+                finish_scalar(done, 2, 2)
+            if done == 0 and phase == 1:
+                round_result(done, 0, N, nc.vector.tensor_copy)
+
+        before, final = TILES - 2, TILES - 1
+        round_lin(last)
+        square(last, 0, 2)
+        square(last, 2, 2)
+        round_result(before, 0, half, nc.vector.tensor_copy)
+        quant_lin(last)
+        mm_lin(last)
+        quant_sq(last - 1)
+        mm_sq(last - 1)
+        round_result(before, half, N, nc.vector.tensor_copy)
+        quant_sq(last, 0, 2)
+        mm_sq(last, 0, 2)
+        quant_result(before, 0, N)
+        quant_sq(last, 2, 2)
+        mm_sq(last, 2, 2)
+        open_result(final)
+        relu_vector(final, 0)
+        relu_scalar(final, 1)
+        finish_scalar(final, 0, 1)
+        finish_scalar(final, 1, 1)
+        relu_vector(final, 2)
+        relu_vector(final, 3)
+        finish_scalar(final, 2, 1)
+        finish_vector(final, 3, 1)
+        round_result(final, 0, half, nc.vector.tensor_copy)
+        round_result(final, half, TAIL_VECTOR_COLS, nc.vector.tensor_copy)
+        round_result(final, TAIL_VECTOR_COLS, N, nc.scalar.copy)
+        quant_result(final, 0, half)
+        quant_result(final, half, N)
+        for q in range(4):
+            queue = nc.sync if q % 2 == 0 else nc.scalar
+            queue.dma_start(
+                out=out_2[:, 4 * q : 4 * q + 4, :].bitcast(I32).rearrange("a r n -> r a n"),
+                in_=res_plane[32 * q : 32 * q + 4, :].bitcast(I32).rearrange("r (a n) -> r a n", a=TILES),
+            )

@@ -20,7 +20,7 @@ SPAN = P * PACK
 PASSES = K // SPAN
 TILES = T // SPAN
 UNITS = PASSES * TILES
-FIRST_PIECES = (128, 128, 256)
+FIRST_PIECES = (512,)
 TAIL_VECTOR_COLS = 320
 W8_ROW = 4
 
@@ -36,18 +36,20 @@ def tile_mix_feat_tm_quadpl_relu2_kernel(
         psum = ctx.enter_context(tc.psum_pool(name="psum", bufs=2))
         ctx.enter_context(tc.manual_schedule())
 
-        w_planes = keep.tile([P, PASSES * N], U8, align_bytes=64)
+        w4_plane = keep.tile([P, PASSES * N], U8, align_bytes=64)
+        w8_plane = keep.tile([P, PASSES * N], U8, align_bytes=64)
         zero_seed = keep.tile([P, 8], F32)
         zero_bias = keep.tile([P, 8], F32)
         nc.vector.memset(zero_seed[:], 0.0)
-        nc.vector.memset(w_planes[:].bitcast(I32), 0)
+        nc.vector.memset(w8_plane[:].bitcast(I32), 0)
+        nc.vector.memset(w4_plane[:].bitcast(I32), 0)
         nc.scalar.activation(out=zero_bias[:], in_=zero_seed[:], func=ACT.Square)
         bias = zero_bias[:, 0:1]
 
-        def load_scales(scales, row0):
+        def load_scales(queue, plane, scales, row0):
             for q in range(4):
-                rows = w_planes[32 * q + row0 : 32 * q + row0 + 4, :]
-                nc.sync.dma_start(
+                rows = plane[32 * q + row0 : 32 * q + row0 + 4, :]
+                queue.dma_start(
                     out=rows.bitcast(I32).rearrange("r (g n) -> r g n", g=PASSES),
                     in_=scales[:, 4 * q : 4 * q + 4, :].bitcast(I32).rearrange("g r n -> r g n"),
                 )
@@ -81,19 +83,13 @@ def tile_mix_feat_tm_quadpl_relu2_kernel(
             nc.sync.dma_start(out=w4[g][:].bitcast(I32), in_=w4_words[g].bitcast(I32))
 
         load_x(0)
-        load_x(1)
-        load_scales(w8_scales, W8_ROW)
-        load_w8(0)
-        load_x(2)
-        load_scales(w4_scales, 0)
-        load_w4(0)
-        load_w8(1)
-        load_x(3)
-        load_w4(1)
-        load_w8(2)
-        load_w4(2)
-        for u in range(4, UNITS):
+        load_scales(nc.gpsimd, w8_plane, w8_scales, W8_ROW)
+        load_scales(nc.scalar, w4_plane, w4_scales, 0)
+        for u in range(1, UNITS):
             load_x(u)
+            if u <= PASSES:
+                load_w8(u - 1)
+                load_w4(u - 1)
 
         lin_bf, sq_bf, lin_q, sq_q, acc, rel, res, res_bf = {}, {}, {}, {}, {}, {}, {}, {}
         res_plane = keep.tile([P, TILES * N], U8, align_bytes=64)
@@ -131,10 +127,10 @@ def tile_mix_feat_tm_quadpl_relu2_kernel(
         def quant_sq(u, r0=0, r_n=PACK):
             sq_q[u, r0] = quantize(sq_bf[u, r0], r_n * P, "sq")
 
-        def mm_lin(u):
+        def mm_lin(u, banks=range(PACK)):
             tile_t, g = divmod(u, PASSES)
             words, plane = lin_q[u]
-            for r in range(PACK):
+            for r in banks:
                 if g == 0:
                     acc[tile_t, r] = psum.tile([P, N], F32, name="acc%d" % r)
                 cols = slice(r * P, (r + 1) * P)
@@ -143,22 +139,22 @@ def tile_mix_feat_tm_quadpl_relu2_kernel(
                     lhsT=words[:, cols].bitcast(FP8X4),
                     lhsT_scale=plane[:, cols],
                     rhs=w8[g][:].bitcast(FP8X4),
-                    rhs_scale=w_planes[W8_ROW:, g * N : (g + 1) * N],
+                    rhs_scale=w8_plane[W8_ROW:, g * N : (g + 1) * N],
                     start=(g == 0),
                     stop=False,
                 )
 
-        def mm_sq(u, r0=0, r_n=PACK):
+        def mm_sq(u, r0=0, banks=range(PACK)):
             tile_t, g = divmod(u, PASSES)
             words, plane = sq_q[u, r0]
-            for r in range(r_n):
-                cols = slice(r * P, (r + 1) * P)
+            for r in banks:
+                cols = slice((r - r0) * P, (r - r0 + 1) * P)
                 nc.tensor.matmul_mx(
-                    out=acc[tile_t, r0 + r][:],
+                    out=acc[tile_t, r][:],
                     lhsT=words[:, cols].bitcast(FP8X4),
                     lhsT_scale=plane[:, cols],
                     rhs=w4[g][:].bitcast(FP4X4),
-                    rhs_scale=w_planes[:, g * N : (g + 1) * N],
+                    rhs_scale=w4_plane[:, g * N : (g + 1) * N],
                     start=False,
                     stop=(g == PASSES - 1),
                 )
@@ -184,14 +180,12 @@ def tile_mix_feat_tm_quadpl_relu2_kernel(
         def finish_scalar(tile_t, r0, r_n):
             cols = slice(r0 * N, (r0 + r_n) * N)
             nc.scalar.activation(out=res[tile_t][:, cols], in_=rel[tile_t][:, cols], func=ACT.Square, bias=bias)
-            store_rows(tile_t, r0, r_n)
 
         def finish_vector(tile_t, r0, r_n):
             cols = slice(r0 * N, (r0 + r_n) * N)
             nc.vector.tensor_tensor(
                 out=res[tile_t][:, cols], in0=rel[tile_t][:, cols], in1=rel[tile_t][:, cols], op=ALU.mult
             )
-            store_rows(tile_t, r0, r_n)
 
         def round_result(tile_t, n0, n1, copy):
             src = res[tile_t][:].rearrange("p (r c e) -> p c r e", r=PACK, e=PACK)
@@ -208,60 +202,98 @@ def tile_mix_feat_tm_quadpl_relu2_kernel(
             rows = out_1[tile_t].rearrange("p n i -> p (n i)").bitcast(I32)
             nc.sync.dma_start(out=rows[:, n0:n1], in_=words[:])
 
-        last = UNITS - 1
         half = N // 2
-        for u in range(last):
-            done = u // PASSES - 1
-            phase = u % PASSES
+        vcopy = nc.vector.tensor_copy
+        for u in range(PASSES):
             round_lin(u)
             square(u)
-            if u > 0:
-                quant_sq(u - 1)
-                mm_sq(u - 1)
-            if done == 0 and phase == 2:
-                quant_result(done, 0, N)
             quant_lin(u)
-            mm_lin(u)
-            if done >= 0 and phase == 0:
-                open_result(done)
-                relu_scalar(done, 0)
-                relu_scalar(done, 1)
-                relu_vector(done, 2)
-                relu_vector(done, 3)
-                finish_scalar(done, 0, 2)
-                finish_scalar(done, 2, 2)
-            if done == 0 and phase == 1:
-                round_result(done, 0, N, nc.vector.tensor_copy)
-
-        before, final = TILES - 2, TILES - 1
-        round_lin(last)
-        square(last, 0, 2)
-        square(last, 2, 2)
-        round_result(before, 0, half, nc.vector.tensor_copy)
-        quant_lin(last)
-        mm_lin(last)
-        quant_sq(last - 1)
-        mm_sq(last - 1)
-        round_result(before, half, N, nc.vector.tensor_copy)
-        quant_sq(last, 0, 2)
-        mm_sq(last, 0, 2)
-        quant_result(before, 0, N)
-        quant_sq(last, 2, 2)
-        mm_sq(last, 2, 2)
-        open_result(final)
-        relu_vector(final, 0)
-        relu_scalar(final, 1)
-        finish_scalar(final, 0, 1)
-        finish_scalar(final, 1, 1)
-        relu_vector(final, 2)
-        relu_vector(final, 3)
-        finish_scalar(final, 2, 1)
-        finish_vector(final, 3, 1)
-        round_result(final, 0, half, nc.vector.tensor_copy)
-        round_result(final, half, TAIL_VECTOR_COLS, nc.vector.tensor_copy)
-        round_result(final, TAIL_VECTOR_COLS, N, nc.scalar.copy)
-        quant_result(final, 0, half)
-        quant_result(final, half, N)
+            quant_sq(u)
+            if u < PASSES - 1:
+                mm_lin(u)
+                mm_sq(u)
+            else:
+                for r in range(PACK):
+                    mm_lin(u, [r])
+                    mm_sq(u, 0, [r])
+        open_result(0)
+        round_lin(3)
+        square(3)
+        relu_vector(0, 0)
+        quant_lin(3)
+        mm_lin(3)
+        relu_vector(0, 1)
+        relu_scalar(0, 2)
+        finish_scalar(0, 0, 1)
+        relu_scalar(0, 3)
+        finish_scalar(0, 1, 1)
+        finish_scalar(0, 2, 2)
+        store_rows(0, 0, PACK)
+        round_lin(4)
+        square(4)
+        quant_sq(3)
+        mm_sq(3)
+        quant_lin(4)
+        mm_lin(4)
+        round_lin(5)
+        square(5)
+        round_result(0, 0, half, vcopy)
+        quant_lin(5)
+        mm_lin(5)
+        round_result(0, half, N, vcopy)
+        quant_sq(4)
+        mm_sq(4)
+        quant_result(0, 0, N)
+        round_lin(6)
+        square(6)
+        quant_sq(5)
+        mm_sq(5)
+        quant_lin(6)
+        mm_lin(6)
+        round_lin(7)
+        open_result(1)
+        relu_scalar(1, 0)
+        relu_scalar(1, 1)
+        square(7)
+        quant_sq(6)
+        mm_sq(6)
+        relu_vector(1, 2)
+        relu_vector(1, 3)
+        quant_lin(7)
+        mm_lin(7)
+        finish_scalar(1, 0, 2)
+        finish_scalar(1, 2, 2)
+        store_rows(1, 0, PACK)
+        round_lin(8)
+        square(8, 0, 2)
+        square(8, 2, 2)
+        quant_sq(7)
+        mm_sq(7)
+        quant_lin(8)
+        mm_lin(8)
+        round_result(1, 0, N, vcopy)
+        quant_sq(8, 0, 2)
+        mm_sq(8, 0, [0, 1])
+        quant_result(1, 0, N)
+        quant_sq(8, 2, 2)
+        mm_sq(8, 2, [2, 3])
+        open_result(2)
+        relu_scalar(2, 0)
+        relu_vector(2, 1)
+        finish_scalar(2, 0, 1)
+        store_rows(2, 0, 1)
+        finish_scalar(2, 1, 1)
+        store_rows(2, 1, 1)
+        relu_vector(2, 2)
+        relu_vector(2, 3)
+        finish_scalar(2, 2, 1)
+        finish_vector(2, 3, 1)
+        store_rows(2, 2, 2)
+        round_result(2, 0, half, vcopy)
+        round_result(2, half, TAIL_VECTOR_COLS, vcopy)
+        round_result(2, TAIL_VECTOR_COLS, N, nc.scalar.copy)
+        quant_result(2, 0, half)
+        quant_result(2, half, N)
         for q in range(4):
             queue = nc.sync if q % 2 == 0 else nc.scalar
             queue.dma_start(

from contextlib import ExitStack

import concourse.mybir as mybir

K, N, T = 1536, 512, 1536
FLOPS = 2 * 2 * K * N * T

F32 = mybir.dt.float32
BF16 = mybir.dt.bfloat16
I32 = mybir.dt.int32
U8 = mybir.dt.uint8
FP8X4 = mybir.dt.float8_e4m3fn_x4
FP4X4 = mybir.dt.float4_e2m1fn_x4
ACT = mybir.ActivationFunctionType
ALU = mybir.AluOpType

P = 128
PACK = 4
SPAN = P * PACK
PASSES = K // SPAN
TILES = T // SPAN
UNITS = PASSES * TILES
FIRST_PIECES = (512,)
TAIL_VECTOR_COLS = 320
W8_ROW = 4


def tile_mix_feat_tm_quadpl_relu2_kernel(
    tc, x, w4_words, w4_scales, w8_words, w8_scales, out_0, out_1, out_2
):
    nc = tc.nc
    with ExitStack() as ctx:
        keep = ctx.enter_context(tc.tile_pool(name="keep", bufs=1))
        stage = ctx.enter_context(tc.tile_pool(name="stage", bufs=3))
        codes_pool = ctx.enter_context(tc.tile_pool(name="codes", bufs=5))
        psum = ctx.enter_context(tc.psum_pool(name="psum", bufs=2))
        ctx.enter_context(tc.manual_schedule())

        w4_plane = keep.tile([P, PASSES * N], U8, align_bytes=64)
        w8_plane = keep.tile([P, PASSES * N], U8, align_bytes=64)
        zero_seed = keep.tile([P, 8], F32)
        zero_bias = keep.tile([P, 8], F32)
        nc.vector.memset(zero_seed[:], 0.0)
        nc.vector.memset(w8_plane[:].bitcast(I32), 0)
        nc.vector.memset(w4_plane[:].bitcast(I32), 0)
        nc.scalar.activation(out=zero_bias[:], in_=zero_seed[:], func=ACT.Square)
        bias = zero_bias[:, 0:1]

        def load_scales(queue, plane, scales, row0):
            for q in range(4):
                rows = plane[32 * q + row0 : 32 * q + row0 + 4, :]
                queue.dma_start(
                    out=rows.bitcast(I32).rearrange("r (g n) -> r g n", g=PASSES),
                    in_=scales[:, 4 * q : 4 * q + 4, :].bitcast(I32).rearrange("g r n -> r g n"),
                )

        raw = {}
        w4 = {}
        w8 = {}

        def load_x(u):
            tile_t, g = divmod(u, PASSES)
            widths = FIRST_PIECES if u == 0 else (SPAN,)
            pieces = []
            c0 = 0
            for n_piece, width in enumerate(widths):
                piece = keep.tile([P, PACK, width], F32, name="x_%d_%d" % (u, n_piece))
                cols = slice(tile_t * SPAN + c0, tile_t * SPAN + c0 + width)
                nc.sync.dma_start(
                    out=piece[:],
                    in_=x[g * SPAN : (g + 1) * SPAN, cols].rearrange("(p j) w -> p j w", j=PACK),
                )
                pieces.append((piece, c0 // PACK, width // PACK))
                c0 = c0 + width
            raw[u] = pieces

        def load_w8(g):
            w8[g] = keep.tile([P, N], I32, name="w8_%d" % g, align_bytes=64)
            nc.sync.dma_start(out=w8[g][:], in_=w8_words[g].rearrange("p n i -> p (n i)").bitcast(I32))

        def load_w4(g):
            w4[g] = keep.tile([P, 2 * N], U8, name="w4_%d" % g, align_bytes=64)
            nc.sync.dma_start(out=w4[g][:].bitcast(I32), in_=w4_words[g].bitcast(I32))

        load_x(0)
        load_scales(nc.gpsimd, w8_plane, w8_scales, W8_ROW)
        load_scales(nc.scalar, w4_plane, w4_scales, 0)
        for u in range(1, UNITS):
            load_x(u)
            if u <= PASSES:
                load_w8(u - 1)
                load_w4(u - 1)

        lin_bf, sq_bf, lin_q, sq_q, acc, rel, res, res_bf = {}, {}, {}, {}, {}, {}, {}, {}
        res_plane = keep.tile([P, TILES * N], U8, align_bytes=64)

        def dealt(dst, banks):
            return dst[:].rearrange("p (r m j) -> p m j r", r=banks, j=PACK)

        def by_group(piece):
            return piece[:].rearrange("p j (m r) -> p m j r", r=PACK)

        def round_lin(u):
            lin_bf[u] = stage.tile([P, PACK * SPAN], BF16, name="lin_bf", align_bytes=64)
            for piece, m0, m_n in raw[u]:
                nc.vector.tensor_copy(out=dealt(lin_bf[u], PACK)[:, m0 : m0 + m_n], in_=by_group(piece))

        def square(u, r0=0, r_n=PACK):
            sq_bf[u, r0] = stage.tile([P, r_n * SPAN], BF16, name="sq_bf", align_bytes=64)
            for piece, m0, m_n in raw[u]:
                nc.scalar.activation(
                    out=dealt(sq_bf[u, r0], r_n)[:, m0 : m0 + m_n],
                    in_=by_group(piece)[:, :, :, r0 : r0 + r_n],
                    func=ACT.Square,
                    bias=bias,
                )

        def quantize(src, width, name):
            words = codes_pool.tile([P, width], I32, name=name + "_words", align_bytes=64)
            plane = codes_pool.tile([P, width], U8, name=name + "_plane", align_bytes=64)
            nc.vector.quantize_mx(out=words[:].bitcast(FP8X4), scales=plane[:], in_=src[:])
            return words, plane

        def quant_lin(u):
            lin_q[u] = quantize(lin_bf[u], SPAN, "lin")

        def quant_sq(u, r0=0, r_n=PACK):
            sq_q[u, r0] = quantize(sq_bf[u, r0], r_n * P, "sq")

        def mm_lin(u, banks=range(PACK)):
            tile_t, g = divmod(u, PASSES)
            words, plane = lin_q[u]
            for r in banks:
                if g == 0:
                    acc[tile_t, r] = psum.tile([P, N], F32, name="acc%d" % r)
                cols = slice(r * P, (r + 1) * P)
                nc.tensor.matmul_mx(
                    out=acc[tile_t, r][:],
                    lhsT=words[:, cols].bitcast(FP8X4),
                    lhsT_scale=plane[:, cols],
                    rhs=w8[g][:].bitcast(FP8X4),
                    rhs_scale=w8_plane[W8_ROW:, g * N : (g + 1) * N],
                    start=(g == 0),
                    stop=False,
                )

        def mm_sq(u, r0=0, banks=range(PACK)):
            tile_t, g = divmod(u, PASSES)
            words, plane = sq_q[u, r0]
            for r in banks:
                cols = slice((r - r0) * P, (r - r0 + 1) * P)
                nc.tensor.matmul_mx(
                    out=acc[tile_t, r][:],
                    lhsT=words[:, cols].bitcast(FP8X4),
                    lhsT_scale=plane[:, cols],
                    rhs=w4[g][:].bitcast(FP4X4),
                    rhs_scale=w4_plane[:, g * N : (g + 1) * N],
                    start=False,
                    stop=(g == PASSES - 1),
                )

        def open_result(tile_t):
            rel[tile_t] = stage.tile([P, PACK * N], F32, name="rel", bufs=2)
            res[tile_t] = keep.tile([P, PACK * N], F32, name="res_%d" % tile_t)
            res_bf[tile_t] = stage.tile([P, PACK * N], BF16, name="res_bf", bufs=2, align_bytes=64)

        def relu_scalar(tile_t, r):
            nc.scalar.activation(out=rel[tile_t][:, r * N : (r + 1) * N], in_=acc[tile_t, r][:], func=ACT.Relu, bias=bias)

        def relu_vector(tile_t, r):
            nc.vector.tensor_scalar(
                out=rel[tile_t][:, r * N : (r + 1) * N], in0=acc[tile_t, r][:], scalar1=0.0, scalar2=None, op0=ALU.max
            )

        def store_rows(tile_t, r0, r_n):
            rows = out_0[tile_t * SPAN : (tile_t + 1) * SPAN, :].rearrange("(p r) n -> p (r n)", r=PACK)
            cols = slice(r0 * N, (r0 + r_n) * N)
            nc.sync.dma_start(out=rows[:, cols], in_=res[tile_t][:, cols])

        def finish_scalar(tile_t, r0, r_n):
            cols = slice(r0 * N, (r0 + r_n) * N)
            nc.scalar.activation(out=res[tile_t][:, cols], in_=rel[tile_t][:, cols], func=ACT.Square, bias=bias)

        def finish_vector(tile_t, r0, r_n):
            cols = slice(r0 * N, (r0 + r_n) * N)
            nc.vector.tensor_tensor(
                out=res[tile_t][:, cols], in0=rel[tile_t][:, cols], in1=rel[tile_t][:, cols], op=ALU.mult
            )

        def round_result(tile_t, n0, n1, copy):
            src = res[tile_t][:].rearrange("p (r c e) -> p c r e", r=PACK, e=PACK)
            dst = res_bf[tile_t][:].rearrange("p (c e r) -> p c r e", r=PACK, e=PACK)
            copy(out=dst[:, n0 // PACK : n1 // PACK], in_=src[:, n0 // PACK : n1 // PACK])

        def quant_result(tile_t, n0, n1):
            words = stage.tile([P, n1 - n0], I32, name="res_words", align_bytes=64)
            nc.vector.quantize_mx(
                out=words[:].bitcast(FP8X4),
                scales=res_plane[:, tile_t * N + n0 : tile_t * N + n1],
                in_=res_bf[tile_t][:, PACK * n0 : PACK * n1],
            )
            rows = out_1[tile_t].rearrange("p n i -> p (n i)").bitcast(I32)
            nc.sync.dma_start(out=rows[:, n0:n1], in_=words[:])

        half = N // 2
        vcopy = nc.vector.tensor_copy
        for u in range(PASSES):
            round_lin(u)
            square(u)
            quant_lin(u)
            quant_sq(u)
            if u < PASSES - 1:
                mm_lin(u)
                mm_sq(u)
            else:
                for r in range(PACK):
                    mm_lin(u, [r])
                    mm_sq(u, 0, [r])
        open_result(0)
        round_lin(3)
        square(3)
        relu_vector(0, 0)
        quant_lin(3)
        mm_lin(3)
        relu_vector(0, 1)
        relu_scalar(0, 2)
        finish_scalar(0, 0, 1)
        relu_scalar(0, 3)
        finish_scalar(0, 1, 1)
        finish_scalar(0, 2, 2)
        store_rows(0, 0, PACK)
        round_lin(4)
        square(4)
        quant_sq(3)
        mm_sq(3)
        quant_lin(4)
        mm_lin(4)
        round_lin(5)
        square(5)
        round_result(0, 0, half, vcopy)
        quant_lin(5)
        mm_lin(5)
        round_result(0, half, N, vcopy)
        quant_sq(4)
        mm_sq(4)
        quant_result(0, 0, N)
        round_lin(6)
        square(6)
        quant_sq(5)
        mm_sq(5)
        quant_lin(6)
        mm_lin(6)
        round_lin(7)
        open_result(1)
        relu_scalar(1, 0)
        relu_scalar(1, 1)
        square(7)
        quant_sq(6)
        mm_sq(6)
        relu_vector(1, 2)
        relu_vector(1, 3)
        quant_lin(7)
        mm_lin(7)
        finish_scalar(1, 0, 2)
        finish_scalar(1, 2, 2)
        store_rows(1, 0, PACK)
        round_lin(8)
        square(8, 0, 2)
        square(8, 2, 2)
        quant_sq(7)
        mm_sq(7)
        quant_lin(8)
        mm_lin(8)
        round_result(1, 0, N, vcopy)
        quant_sq(8, 0, 2)
        mm_sq(8, 0, [0, 1])
        quant_result(1, 0, N)
        quant_sq(8, 2, 2)
        mm_sq(8, 2, [2, 3])
        open_result(2)
        relu_scalar(2, 0)
        relu_vector(2, 1)
        finish_scalar(2, 0, 1)
        store_rows(2, 0, 1)
        finish_scalar(2, 1, 1)
        store_rows(2, 1, 1)
        relu_vector(2, 2)
        relu_vector(2, 3)
        finish_scalar(2, 2, 1)
        finish_vector(2, 3, 1)
        store_rows(2, 2, 2)
        round_result(2, 0, half, vcopy)
        round_result(2, half, TAIL_VECTOR_COLS, vcopy)
        round_result(2, TAIL_VECTOR_COLS, N, nc.scalar.copy)
        quant_result(2, 0, half)
        quant_result(2, half, N)
        for q in range(4):
            queue = nc.sync if q % 2 == 0 else nc.scalar
            queue.dma_start(
                out=out_2[:, 4 * q : 4 * q + 4, :].bitcast(I32).rearrange("a r n -> r a n"),
                in_=res_plane[32 * q : 32 * q + 4, :].bitcast(I32).rearrange("r (a n) -> r a n", a=TILES),
            )
